import numpy as np, ml_dtypes
CORES = [16,17,18,19,150,151]
N = 6
import mx_ref
NC = 384
BF = ml_dtypes.bfloat16
def setup_inputs(rng):
    def f(*shape):
        return mx_ref.flush((rng.standard_normal(shape, dtype=np.float32) * np.exp2(rng.integers(-2, 3, shape[:-1] + (1,)))).astype(BF))
    return {"x": f(N, 128, 512), "w": f(N, 128, 4 * NC)}
def setup_inputs_blocks(rng):
    d = setup_inputs(rng)
    for k in ("x", "w"): d[k] = mx_ref.spread(d[k], rng, 4)
    return d
def setup_inputs_wide(rng):
    d = setup_inputs(rng)
    for k in ("x", "w"): d[k] = mx_ref.flush((d[k].astype(np.float32) * np.exp2(rng.integers(-6, 7, (N, 1, 1))).astype(np.float32)).astype(BF))
    return d
def setup_inputs_near(rng):
    d = setup_inputs(rng); v = d["w"].astype(np.float32).reshape(N, 128, -1, 4)
    d["w"] = mx_ref.flush((v[:1, :, :1] + v / 64).reshape(d["w"].shape).astype(BF))
    return d
def setup_inputs_twins(rng):
    d = setup_inputs(rng); v = d["w"].reshape(N, 128, -1, 4).copy(); a, b = rng.permutation(N)[:2]; i, j, k = rng.integers(0, v.shape[2], 3)
    v[a, :, i] = (v[a, :, i].astype(np.float32) * 8).astype(BF); v[a, :, j] = v[a, :, i]; v[b, :, k] = v[a, :, i]
    d["w"] = v.reshape(d["w"].shape)
    return d
def reference(x, w):
    W = [mx_ref.quantize(w[r]) for r in range(N)]
    y = np.zeros((N, 128, 2), np.float32)
    for j in range(N):
        X = mx_ref.quantize(x[j])
        L = np.concatenate([mx_ref.matmul(X, W[r]) for r in range(N)], axis=1)
        y[j][:, 0] = L.max(axis=1); y[j][:, 1] = L.argmax(axis=1)
    return {"y": y}

@@ -1,0 +1,164 @@
+from concourse.bass import DstId, RemoteDMATransfer
+from concourse.mybir import dt, AluOpType, ActivationFunctionType, AxisListType
+
+N = 6
+NC = 384
+TOK = 128
+SLOT = 4
+LOW = -1e29
+FAR_INDEX = 8192.0
+
+SCRATCH = {
+    "xin": ("sbuf", [128, 4 * TOK], "bfloat16"),
+    "win": ("sbuf", [128, 4 * NC], "bfloat16"),
+    "wc": ("sbuf", [128, NC], "float8_e4m3fn_x4"),
+    "wp": ("sbuf", [128, NC], "uint8"),
+    "low": ("sbuf", [128, NC], "float32"),
+    "offs": ("sbuf", [128, N], "float32"),
+    "land": ("sbuf", [128, SLOT * N], "float32"),
+    "gidx": ("sbuf", [128, N], "float32"),
+    "lose": ("sbuf", [128, N], "float32"),
+    "fin": ("sbuf", [128, 2 * N], "float32"),
+    "ps": ("psum", [128, 512 * N], "float32"),
+}
+SEMAPHORES = ["ldx", "ldw", "qx", "qw", "setup", "offd", "sent", "own", "res", "f0", "f1", "f2", "f3", "stored"]
+for _j in range(N):
+    SCRATCH["xc%d" % _j] = ("sbuf", [128, TOK], "float8_e4m3fn_x4")
+    SCRATCH["xp%d" % _j] = ("sbuf", [128, TOK], "uint8")
+    SCRATCH["run%d" % _j] = ("sbuf", [128, NC + 4], "float32")
+    SCRATCH["sgn%d" % _j] = ("sbuf", [128, NC], "bfloat16")
+    SEMAPHORES += ["x%d" % _j, "mm%d" % _j, "sc%d" % _j, "ac%d" % _j]
+
+
+def bits(mask):
+    return [b for b in range(16) if mask >> b & 1]
+
+
+def pick(engines):
+    return sum(1 << b for b in engines)
+
+
+def on_chip(topo, a, b):
+    return topo.host(a) == topo.host(b) and topo.chip(a) == topo.chip(b)
+
+
+def plan(topo, cores, r):
+    me = cores[r]
+    others = [(r + k) % N for k in range(1, N)]
+    near = [j for j in others if on_chip(topo, me, cores[j])]
+    far = [j for j in others if j not in near]
+    fmask, nmask = 0xFFFF, 0xFFFF
+    for j in far:
+        fmask &= topo.mask(me, cores[j])
+    for j in near:
+        nmask &= topo.mask(me, cores[j])
+    fe = bits(fmask)
+    ne = [b for b in bits(nmask) if b not in fe]
+    if len(near) == 1:
+        ne = ne[:4]
+    return near, far, ne, fe
+
+
+def result_calls(near, ne, fe):
+    if len(near) == 1:
+        return [[(near[0], ne)]]
+    pool = ne + fe
+    w = 4
+    return [[(j, pool[w * k:w * k + w]) for k, j in enumerate(near)]]
+
+
+def rank_program(g, core, T, topo):
+    r = T.rank_of(core)
+    if r is None:
+        return
+    cores = list(T.cores)
+    near, far, ne, fe = plan(topo, cores, r)
+    v, s, te, sy = g.vector, g.scalar, g.tensor, g.sync
+    sem = T.sem
+    order = [r] + near + far
+
+    def dst(j):
+        rid, pid = topo.addr(cores[j], core)
+        return DstId(rid=rid, pnc=pid)
+
+    sy.dma_start(T.xin[:], T.x[:]).then_inc(sem.ldx, 16)
+    sy.dma_start(T.win[:], T.w[:]).then_inc(sem.ldw, 16)
+
+    v.memset(T.low[:], LOW).then_inc(sem.setup, 1)
+    g.iota(T.offs[:], [[-NC, N]], NC * (N - 1), 0, allow_small_or_imprecise_dtypes=True).then_inc(sem.offd, 1)
+
+    v.wait_ge(sem.ldx, 16)
+    v.quantize_mx(T["xc%d" % r][:], T["xp%d" % r][:], T.xin[:]).then_inc(sem.qx, 1)
+    v.wait_ge(sem.ldw, 16)
+    v.quantize_mx(T.wc[:], T.wp[:], T.win[:]).then_inc(sem.qw, 1)
+
+    g.wait_ge(sem.qx, 1)
+    sent = 0
+    for view in (T["xc%d" % r][:].bitcast(dt.uint8), T["xp%d" % r][:]):
+        trs = []
+        for js, eng in ((far, fe), (near, ne)):
+            trs.append(RemoteDMATransfer(dst_ids=[dst(j) for j in js], dma_engine_mask=pick(eng),
+                                         remote_sem=sem["x%d" % r], srcs=[view], dsts=[view for j in js]))
+            sent += len(eng)
+        g.remote_dma_fused(trs, local_sem=sem.sent)
+
+    te.wait_ge(sem.qw, 1)
+    te.wait_ge(sem.qx, 1)
+    for j in order:
+        if j != r:
+            jnear, jfar, jne, jfe = plan(topo, cores, j)
+            te.wait_ge(sem["x%d" % j], 2 * len(jne if r in jnear else jfe))
+        te.matmul_mx(T.ps[:, 512 * j:512 * j + NC], T["xc%d" % j][:], T["xp%d" % j][:], T.wc[:], T.wp[:],
+                     True, True).then_inc(sem["mm%d" % j], 1)
+
+    v.wait_ge(sem.setup, 1)
+    for j in order:
+        run = T["run%d" % j]
+        v.wait_ge(sem["mm%d" % j], 1)
+        v.tensor_tensor_scan(run[:, 0:NC], T.ps[:, 512 * j:512 * j + NC], T.low[:], LOW,
+                             AluOpType.max, AluOpType.max).then_inc(sem["sc%d" % j], 1)
+        s.wait_ge(sem["sc%d" % j], 1)
+        s.activation(T["sgn%d" % j][:], run[:, 0:NC], ActivationFunctionType.Sign, bias=run[:, NC - 1:NC],
+                     scale=-1.0, accum_out=run[:, NC:NC + 1]).then_inc(sem["ac%d" % j], 1)
+
+    calls = result_calls(near, ne, fe) + [[(j, fe)] for j in far]
+    for call in calls:
+        trs = []
+        for j, eng in call:
+            p = N - 1 - r
+            g.wait_ge(sem["ac%d" % j], 1)
+            trs.append(RemoteDMATransfer(dst_ids=[dst(j)], dma_engine_mask=pick(eng), remote_sem=sem.res,
+                                         srcs=[T["run%d" % j][:, NC - 1:NC + 1]],
+                                         dsts=[T.land[:, SLOT * p:SLOT * p + 2]]))
+            sent += len(eng)
+        g.remote_dma_fused(trs, local_sem=sem.sent)
+
+    p = N - 1 - r
+    v.wait_ge(sem["ac%d" % r], 1)
+    v.tensor_copy(T.land[:, SLOT * p:SLOT * p + 2], T["run%d" % r][:, NC - 1:NC + 1]).then_inc(sem.own, 1)
+
+    due = 0
+    for j in near + far:
+        jnear, jfar, jne, jfe = plan(topo, cores, j)
+        if r in jfar:
+            due += len(jfe)
+        else:
+            due += sum(len(eng) for call in result_calls(jnear, jne, jfe) for k, eng in call if k == r)
+    mx = T.land[:, 0:SLOT * N:SLOT]
+    ix = T.land[:, 1:SLOT * N:SLOT]
+    best = T.fin[:, 2 * N - 3:2 * N - 2]
+    v.wait_ge(sem.offd, 1)
+    v.wait_ge(sem.own, 1)
+    v.wait_ge(sem.res, due)
+    v.tensor_reduce(best, mx, AxisListType.X, AluOpType.max).then_inc(sem.f0, 1)
+    v.tensor_tensor(T.gidx[:], ix, T.offs[:], AluOpType.add).then_inc(sem.f1, 1)
+    v.wait_ge(sem.f0, 1)
+    v.tensor_scalar(T.lose[:], mx, best, FAR_INDEX, AluOpType.is_lt, AluOpType.mult).then_inc(sem.f2, 1)
+    v.wait_ge(sem.f1, 1)
+    v.wait_ge(sem.f2, 1)
+    v.tensor_tensor_scan(T.fin[:, 0:2 * N:2], T.lose[:], T.gidx[:], 0.0, AluOpType.min, AluOpType.max).then_inc(sem.f3, 1)
+    sy.wait_ge(sem.f3, 1)
+    sy.wait_ge(sem.f0, 1)
+    sy.dma_start(T.y[:], T.fin[:, 2 * N - 3:2 * N - 1]).then_inc(sem.stored, 16)
+    sy.wait_ge(sem.stored, 16)
+    g.wait_ge(sem.sent, sent)

@@ -4,28 +4,29 @@ from concourse.mybir import dt, AluOpType, ActivationFunctionType, AxisListType
 N = 6
 NC = 384
 TOK = 128
-SLOT = 4
+STEP = 4
+END = STEP * (NC - 1)
 LOW = -1e29
 FAR_INDEX = 8192.0
 
 SCRATCH = {
     "xin": ("sbuf", [128, 4 * TOK], "bfloat16"),
     "win": ("sbuf", [128, 4 * NC], "bfloat16"),
-    "wc": ("sbuf", [128, NC], "float8_e4m3fn_x4"),
-    "wp": ("sbuf", [128, NC], "uint8"),
     "low": ("sbuf", [128, NC], "float32"),
     "offs": ("sbuf", [128, N], "float32"),
-    "land": ("sbuf", [128, SLOT * N], "float32"),
+    "land": ("sbuf", [128, 2 * N], "float32"),
     "gidx": ("sbuf", [128, N], "float32"),
     "lose": ("sbuf", [128, N], "float32"),
     "fin": ("sbuf", [128, 2 * N], "float32"),
     "ps": ("psum", [128, 512 * N], "float32"),
 }
-SEMAPHORES = ["ldx", "ldw", "qx", "qw", "setup", "offd", "sent", "own", "res", "f0", "f1", "f2", "f3", "stored"]
+SEMAPHORES = ["ldx", "ldw", "qx", "qw", "setup", "offd", "sent", "own", "res", "wn", "f0", "f1", "f2", "f3", "stored"]
 for _j in range(N):
     SCRATCH["xc%d" % _j] = ("sbuf", [128, TOK], "float8_e4m3fn_x4")
     SCRATCH["xp%d" % _j] = ("sbuf", [128, TOK], "uint8")
-    SCRATCH["run%d" % _j] = ("sbuf", [128, NC + 4], "float32")
+    SCRATCH["wc%d" % _j] = ("sbuf", [128, NC], "float8_e4m3fn_x4")
+    SCRATCH["wp%d" % _j] = ("sbuf", [128, NC], "uint8")
+    SCRATCH["run%d" % _j] = ("sbuf", [128, END + 4], "float32")
     SCRATCH["sgn%d" % _j] = ("sbuf", [128, NC], "bfloat16")
     SEMAPHORES += ["x%d" % _j, "mm%d" % _j, "sc%d" % _j, "ac%d" % _j]
 
@@ -44,27 +45,17 @@ def on_chip(topo, a, b):
 
 def plan(topo, cores, r):
     me = cores[r]
-    others = [(r + k) % N for k in range(1, N)]
+    others = [j for j in range(N) if j != r and j % 2 == r % 2]
     near = [j for j in others if on_chip(topo, me, cores[j])]
     far = [j for j in others if j not in near]
-    fmask, nmask = 0xFFFF, 0xFFFF
+    fmask = 0xFFFF
     for j in far:
         fmask &= topo.mask(me, cores[j])
-    for j in near:
-        nmask &= topo.mask(me, cores[j])
+    every = bits(topo.mask(me, cores[r ^ 1]))
     fe = bits(fmask)
-    ne = [b for b in bits(nmask) if b not in fe]
-    if len(near) == 1:
-        ne = ne[:4]
-    return near, far, ne, fe
-
-
-def result_calls(near, ne, fe):
-    if len(near) == 1:
-        return [[(near[0], ne)]]
-    pool = ne + fe
-    w = 4
-    return [[(j, pool[w * k:w * k + w]) for k, j in enumerate(near)]]
+    ne = [b for b in every if b not in fe]
+    we = every if near else ne
+    return {"near": near, "far": far, "ne": ne, "fe": fe, "we": we, "every": every}
 
 
 def rank_program(g, core, T, topo):
@@ -72,10 +63,12 @@ def rank_program(g, core, T, topo):
     if r is None:
         return
     cores = list(T.cores)
-    near, far, ne, fe = plan(topo, cores, r)
+    o = r ^ 1
+    plans = [plan(topo, cores, j) for j in range(N)]
+    me = plans[r]
+    near, far = me["near"], me["far"]
     v, s, te, sy = g.vector, g.scalar, g.tensor, g.sync
     sem = T.sem
-    order = [r] + near + far
 
     def dst(j):
         rid, pid = topo.addr(cores[j], core)
@@ -90,62 +83,73 @@ def rank_program(g, core, T, topo):
     v.wait_ge(sem.ldx, 16)
     v.quantize_mx(T["xc%d" % r][:], T["xp%d" % r][:], T.xin[:]).then_inc(sem.qx, 1)
     v.wait_ge(sem.ldw, 16)
-    v.quantize_mx(T.wc[:], T.wp[:], T.win[:]).then_inc(sem.qw, 1)
+    v.quantize_mx(T["wc%d" % r][:], T["wp%d" % r][:], T.win[:]).then_inc(sem.qw, 1)
 
     g.wait_ge(sem.qx, 1)
     sent = 0
     for view in (T["xc%d" % r][:].bitcast(dt.uint8), T["xp%d" % r][:]):
         trs = []
-        for js, eng in ((far, fe), (near, ne)):
-            trs.append(RemoteDMATransfer(dst_ids=[dst(j) for j in js], dma_engine_mask=pick(eng),
-                                         remote_sem=sem["x%d" % r], srcs=[view], dsts=[view for j in js]))
-            sent += len(eng)
+        for js, eng in ((far, me["fe"]), (near, me["ne"])):
+            if js:
+                trs.append(RemoteDMATransfer(dst_ids=[dst(j) for j in js], dma_engine_mask=pick(eng),
+                                             remote_sem=sem["x%d" % r], srcs=[view], dsts=[view for j in js]))
+                sent += len(eng)
+        g.remote_dma_fused(trs, local_sem=sem.sent)
+    g.wait_ge(sem.qw, 1)
+    for view in (T["wc%d" % r][:].bitcast(dt.uint8), T["wp%d" % r][:]):
+        trs = [RemoteDMATransfer(dst_ids=[dst(o)], dma_engine_mask=pick(me["we"]), remote_sem=sem.wn,
+                                 srcs=[view], dsts=[view])]
+        sent += len(me["we"])
         g.remote_dma_fused(trs, local_sem=sem.sent)
 
-    te.wait_ge(sem.qw, 1)
+    if near:
+        order = [(r, r)] + [(j, r) for j in near] + [(j, o) for j in near]
+        order += [(j, k) for j in far for k in (r, o)] + [(r, o)]
+    else:
+        order = [(r, r)] + [(j, r) for j in far] + [(j, o) for j in far] + [(r, o)]
+
     te.wait_ge(sem.qx, 1)
-    for j in order:
-        if j != r:
-            jnear, jfar, jne, jfe = plan(topo, cores, j)
-            te.wait_ge(sem["x%d" % j], 2 * len(jne if r in jnear else jfe))
-        te.matmul_mx(T.ps[:, 512 * j:512 * j + NC], T["xc%d" % j][:], T["xp%d" % j][:], T.wc[:], T.wp[:],
-                     True, True).then_inc(sem["mm%d" % j], 1)
+    te.wait_ge(sem.qw, 1)
+    seen = [r]
+    swapped = False
+    for i, (j, k) in enumerate(order):
+        if j not in seen:
+            seen.append(j)
+            te.wait_ge(sem["x%d" % j], 2 * len(plans[j]["ne"] if r in plans[j]["near"] else plans[j]["fe"]))
+        if k == o and not swapped:
+            swapped = True
+            te.wait_ge(sem.wn, 2 * len(plans[o]["we"]))
+        te.matmul_mx(T.ps[:, 512 * i:512 * i + NC], T["xc%d" % j][:], T["xp%d" % j][:], T["wc%d" % k][:], T["wp%d" % k][:],
+                     True, True).then_inc(sem["mm%d" % i], 1)
 
     v.wait_ge(sem.setup, 1)
-    for j in order:
+    for i, (j, k) in enumerate(order):
         run = T["run%d" % j]
-        v.wait_ge(sem["mm%d" % j], 1)
-        v.tensor_tensor_scan(run[:, 0:NC], T.ps[:, 512 * j:512 * j + NC], T.low[:], LOW,
-                             AluOpType.max, AluOpType.max).then_inc(sem["sc%d" % j], 1)
-        s.wait_ge(sem["sc%d" % j], 1)
-        s.activation(T["sgn%d" % j][:], run[:, 0:NC], ActivationFunctionType.Sign, bias=run[:, NC - 1:NC],
-                     scale=-1.0, accum_out=run[:, NC:NC + 1]).then_inc(sem["ac%d" % j], 1)
+        at = 2 * (1 - k % 2)
+        last = at + END
+        view = run[:, at:last + 1:STEP]
+        v.wait_ge(sem["mm%d" % i], 1)
+        v.tensor_tensor_scan(view, T.ps[:, 512 * i:512 * i + NC], T.low[:], LOW,
+                             AluOpType.max, AluOpType.max).then_inc(sem["sc%d" % i], 1)
+        s.wait_ge(sem["sc%d" % i], 1)
+        s.activation(T["sgn%d" % i][:], view, ActivationFunctionType.Sign, bias=run[:, last:last + 1],
+                     scale=-1.0, accum_out=run[:, last + 1:last + 2]).then_inc(sem["ac%d" % j], 1)
 
-    calls = result_calls(near, ne, fe) + [[(j, fe)] for j in far]
-    for call in calls:
-        trs = []
-        for j, eng in call:
-            p = N - 1 - r
-            g.wait_ge(sem["ac%d" % j], 1)
-            trs.append(RemoteDMATransfer(dst_ids=[dst(j)], dma_engine_mask=pick(eng), remote_sem=sem.res,
-                                         srcs=[T["run%d" % j][:, NC - 1:NC + 1]],
-                                         dsts=[T.land[:, SLOT * p:SLOT * p + 2]]))
-            sent += len(eng)
+    p = 4 * (N // 2 - 1 - r // 2)
+    for j in near + far:
+        eng = me["every"] if j in near else me["fe"]
+        g.wait_ge(sem["ac%d" % j], 2)
+        trs = [RemoteDMATransfer(dst_ids=[dst(j)], dma_engine_mask=pick(eng), remote_sem=sem.res,
+                                 srcs=[T["run%d" % j][:, END:END + 4]], dsts=[T.land[:, p:p + 4]])]
+        sent += len(eng)
         g.remote_dma_fused(trs, local_sem=sem.sent)
 
-    p = N - 1 - r
-    v.wait_ge(sem["ac%d" % r], 1)
-    v.tensor_copy(T.land[:, SLOT * p:SLOT * p + 2], T["run%d" % r][:, NC - 1:NC + 1]).then_inc(sem.own, 1)
+    v.wait_ge(sem["ac%d" % r], 2)
+    v.tensor_copy(T.land[:, p:p + 4], T["run%d" % r][:, END:END + 4]).then_inc(sem.own, 1)
 
-    due = 0
-    for j in near + far:
-        jnear, jfar, jne, jfe = plan(topo, cores, j)
-        if r in jfar:
-            due += len(jfe)
-        else:
-            due += sum(len(eng) for call in result_calls(jnear, jne, jfe) for k, eng in call if k == r)
-    mx = T.land[:, 0:SLOT * N:SLOT]
-    ix = T.land[:, 1:SLOT * N:SLOT]
+    due = sum(len(plans[j]["every"] if r in plans[j]["near"] else plans[j]["fe"]) for j in near + far)
+    mx = T.land[:, 0:2 * N:2]
+    ix = T.land[:, 1:2 * N:2]
     best = T.fin[:, 2 * N - 3:2 * N - 2]
     v.wait_ge(sem.offd, 1)
     v.wait_ge(sem.own, 1)

from concourse.bass import DstId, RemoteDMATransfer
from concourse.mybir import dt, AluOpType, ActivationFunctionType, AxisListType

N = 6
NC = 384
TOK = 128
STEP = 4
END = STEP * (NC - 1)
LOW = -1e29
FAR_INDEX = 8192.0

SCRATCH = {
    "xin": ("sbuf", [128, 4 * TOK], "bfloat16"),
    "win": ("sbuf", [128, 4 * NC], "bfloat16"),
    "low": ("sbuf", [128, NC], "float32"),
    "offs": ("sbuf", [128, N], "float32"),
    "land": ("sbuf", [128, 2 * N], "float32"),
    "gidx": ("sbuf", [128, N], "float32"),
    "lose": ("sbuf", [128, N], "float32"),
    "fin": ("sbuf", [128, 2 * N], "float32"),
    "ps": ("psum", [128, 512 * N], "float32"),
}
SEMAPHORES = ["ldx", "ldw", "qx", "qw", "setup", "offd", "sent", "own", "res", "wn", "f0", "f1", "f2", "f3", "stored"]
for _j in range(N):
    SCRATCH["xc%d" % _j] = ("sbuf", [128, TOK], "float8_e4m3fn_x4")
    SCRATCH["xp%d" % _j] = ("sbuf", [128, TOK], "uint8")
    SCRATCH["wc%d" % _j] = ("sbuf", [128, NC], "float8_e4m3fn_x4")
    SCRATCH["wp%d" % _j] = ("sbuf", [128, NC], "uint8")
    SCRATCH["run%d" % _j] = ("sbuf", [128, END + 4], "float32")
    SCRATCH["sgn%d" % _j] = ("sbuf", [128, NC], "bfloat16")
    SEMAPHORES += ["x%d" % _j, "mm%d" % _j, "sc%d" % _j, "ac%d" % _j]


def bits(mask):
    return [b for b in range(16) if mask >> b & 1]


def pick(engines):
    return sum(1 << b for b in engines)


def on_chip(topo, a, b):
    return topo.host(a) == topo.host(b) and topo.chip(a) == topo.chip(b)


def plan(topo, cores, r):
    me = cores[r]
    others = [j for j in range(N) if j != r and j % 2 == r % 2]
    near = [j for j in others if on_chip(topo, me, cores[j])]
    far = [j for j in others if j not in near]
    fmask = 0xFFFF
    for j in far:
        fmask &= topo.mask(me, cores[j])
    every = bits(topo.mask(me, cores[r ^ 1]))
    fe = bits(fmask)
    ne = [b for b in every if b not in fe]
    we = every if near else ne
    return {"near": near, "far": far, "ne": ne, "fe": fe, "we": we, "every": every}


def rank_program(g, core, T, topo):
    r = T.rank_of(core)
    if r is None:
        return
    cores = list(T.cores)
    o = r ^ 1
    plans = [plan(topo, cores, j) for j in range(N)]
    me = plans[r]
    near, far = me["near"], me["far"]
    v, s, te, sy = g.vector, g.scalar, g.tensor, g.sync
    sem = T.sem

    def dst(j):
        rid, pid = topo.addr(cores[j], core)
        return DstId(rid=rid, pnc=pid)

    sy.dma_start(T.xin[:], T.x[:]).then_inc(sem.ldx, 16)
    sy.dma_start(T.win[:], T.w[:]).then_inc(sem.ldw, 16)

    v.memset(T.low[:], LOW).then_inc(sem.setup, 1)
    g.iota(T.offs[:], [[-NC, N]], NC * (N - 1), 0, allow_small_or_imprecise_dtypes=True).then_inc(sem.offd, 1)

    v.wait_ge(sem.ldx, 16)
    v.quantize_mx(T["xc%d" % r][:], T["xp%d" % r][:], T.xin[:]).then_inc(sem.qx, 1)
    v.wait_ge(sem.ldw, 16)
    v.quantize_mx(T["wc%d" % r][:], T["wp%d" % r][:], T.win[:]).then_inc(sem.qw, 1)

    g.wait_ge(sem.qx, 1)
    sent = 0
    for view in (T["xc%d" % r][:].bitcast(dt.uint8), T["xp%d" % r][:]):
        trs = []
        for js, eng in ((far, me["fe"]), (near, me["ne"])):
            if js:
                trs.append(RemoteDMATransfer(dst_ids=[dst(j) for j in js], dma_engine_mask=pick(eng),
                                             remote_sem=sem["x%d" % r], srcs=[view], dsts=[view for j in js]))
                sent += len(eng)
        g.remote_dma_fused(trs, local_sem=sem.sent)
    g.wait_ge(sem.qw, 1)
    for view in (T["wc%d" % r][:].bitcast(dt.uint8), T["wp%d" % r][:]):
        trs = [RemoteDMATransfer(dst_ids=[dst(o)], dma_engine_mask=pick(me["we"]), remote_sem=sem.wn,
                                 srcs=[view], dsts=[view])]
        sent += len(me["we"])
        g.remote_dma_fused(trs, local_sem=sem.sent)

    if near:
        order = [(r, r)] + [(j, r) for j in near] + [(j, o) for j in near]
        order += [(j, k) for j in far for k in (r, o)] + [(r, o)]
    else:
        order = [(r, r)] + [(j, r) for j in far] + [(j, o) for j in far] + [(r, o)]

    te.wait_ge(sem.qx, 1)
    te.wait_ge(sem.qw, 1)
    seen = [r]
    swapped = False
    for i, (j, k) in enumerate(order):
        if j not in seen:
            seen.append(j)
            te.wait_ge(sem["x%d" % j], 2 * len(plans[j]["ne"] if r in plans[j]["near"] else plans[j]["fe"]))
        if k == o and not swapped:
            swapped = True
            te.wait_ge(sem.wn, 2 * len(plans[o]["we"]))
        te.matmul_mx(T.ps[:, 512 * i:512 * i + NC], T["xc%d" % j][:], T["xp%d" % j][:], T["wc%d" % k][:], T["wp%d" % k][:],
                     True, True).then_inc(sem["mm%d" % i], 1)

    v.wait_ge(sem.setup, 1)
    for i, (j, k) in enumerate(order):
        run = T["run%d" % j]
        at = 2 * (1 - k % 2)
        last = at + END
        view = run[:, at:last + 1:STEP]
        v.wait_ge(sem["mm%d" % i], 1)
        v.tensor_tensor_scan(view, T.ps[:, 512 * i:512 * i + NC], T.low[:], LOW,
                             AluOpType.max, AluOpType.max).then_inc(sem["sc%d" % i], 1)
        s.wait_ge(sem["sc%d" % i], 1)
        s.activation(T["sgn%d" % i][:], view, ActivationFunctionType.Sign, bias=run[:, last:last + 1],
                     scale=-1.0, accum_out=run[:, last + 1:last + 2]).then_inc(sem["ac%d" % j], 1)

    p = 4 * (N // 2 - 1 - r // 2)
    for j in near + far:
        eng = me["every"] if j in near else me["fe"]
        g.wait_ge(sem["ac%d" % j], 2)
        trs = [RemoteDMATransfer(dst_ids=[dst(j)], dma_engine_mask=pick(eng), remote_sem=sem.res,
                                 srcs=[T["run%d" % j][:, END:END + 4]], dsts=[T.land[:, p:p + 4]])]
        sent += len(eng)
        g.remote_dma_fused(trs, local_sem=sem.sent)

    v.wait_ge(sem["ac%d" % r], 2)
    v.tensor_copy(T.land[:, p:p + 4], T["run%d" % r][:, END:END + 4]).then_inc(sem.own, 1)

    due = sum(len(plans[j]["every"] if r in plans[j]["near"] else plans[j]["fe"]) for j in near + far)
    mx = T.land[:, 0:2 * N:2]
    ix = T.land[:, 1:2 * N:2]
    best = T.fin[:, 2 * N - 3:2 * N - 2]
    v.wait_ge(sem.offd, 1)
    v.wait_ge(sem.own, 1)
    v.wait_ge(sem.res, due)
    v.tensor_reduce(best, mx, AxisListType.X, AluOpType.max).then_inc(sem.f0, 1)
    v.tensor_tensor(T.gidx[:], ix, T.offs[:], AluOpType.add).then_inc(sem.f1, 1)
    v.wait_ge(sem.f0, 1)
    v.tensor_scalar(T.lose[:], mx, best, FAR_INDEX, AluOpType.is_lt, AluOpType.mult).then_inc(sem.f2, 1)
    v.wait_ge(sem.f1, 1)
    v.wait_ge(sem.f2, 1)
    v.tensor_tensor_scan(T.fin[:, 0:2 * N:2], T.lose[:], T.gidx[:], 0.0, AluOpType.min, AluOpType.max).then_inc(sem.f3, 1)
    sy.wait_ge(sem.f3, 1)
    sy.wait_ge(sem.f0, 1)
    sy.dma_start(T.y[:], T.fin[:, 2 * N - 3:2 * N - 1]).then_inc(sem.stored, 16)
    sy.wait_ge(sem.stored, 16)
    g.wait_ge(sem.sent, sent)
